import numpy as np
import ml_dtypes


def mxq(x, axis, fmt="e4m3"):
    dtype, down = {"e4m3": (ml_dtypes.float8_e4m3fn, 7), "e5m2": (ml_dtypes.float8_e5m2, 14)}[fmt]
    v = np.moveaxis(np.asarray(x, np.float32).astype(ml_dtypes.bfloat16).astype(np.float64), axis, -1)
    blocks = v.reshape(v.shape[:-1] + (-1, 32))
    amax = np.abs(blocks).max(-1, keepdims=True)
    byte = np.maximum(np.where(amax > 0, np.frexp(amax)[1] - 1 + 127, 0) - down, 1)
    scale = np.exp2(byte - 127.0)
    codes = (blocks / scale).astype(np.float32).astype(dtype).astype(np.float64)
    return np.moveaxis((codes * scale).reshape(v.shape), -1, axis)


WIDE = False


def mx_kscale(k):
    if not WIDE:
        return np.ones(k)
    levels = np.array([10, -10, 5, -5, 0])
    if k % 512:
        return np.exp2(np.random.permutation(np.resize(levels, k // 32))).repeat(32)
    a = np.empty((k // 512, 16))
    for p in range(k // 512):
        a[p, :8] = np.random.permutation(np.resize(levels, 8))
        for g in range(8):
            far = levels[np.abs(levels - a[p, g]) >= 10]
            a[p, g + 8] = far[np.random.randint(len(far))]
    return np.exp2(a.ravel()).repeat(32)


BF16 = ml_dtypes.bfloat16


def bf(x):
    return np.asarray(x, np.float32).astype(BF16)


def f64(x):
    return np.asarray(x).astype(np.float64)


E2M1 = np.array([0.0, 0.5, 1.0, 1.5, 2.0, 3.0, 4.0, 6.0, -0.0, -0.5, -1.0, -1.5, -2.0, -3.0, -4.0, -6.0])


def pack_weight(w, fmt):
    k, n = w.shape
    w = f64(bf(w)).reshape(k // 32, 32, n)
    amax = np.abs(w).max(1)
    if fmt == "e4m3":
        byte = np.frexp(amax)[1] - 1 + 127 - 7
    else:
        mant, ex = np.frexp(amax / 6.0)
        byte = np.where(mant > 0.5, ex, ex - 1) + 127
    byte = np.clip(np.where(amax > 0, byte, 1), 1, 254)
    scaled = (w * np.exp2(127.0 - byte)[:, None, :]).reshape(k, n).astype(np.float32)
    by_word = np.ascontiguousarray(scaled.reshape(k // 512, 128, 4, n).transpose(0, 1, 3, 2))
    if fmt == "e4m3":
        words = by_word.astype(ml_dtypes.float8_e4m3fn).view(np.uint8)
    else:
        c = by_word.astype(ml_dtypes.float4_e2m1fn).view(np.uint8) & 0xF
        words = c[..., 0::2] | (c[..., 1::2] << 4)
    return np.ascontiguousarray(words), np.ascontiguousarray(byte.astype(np.uint8).reshape(k // 512, 16, n))


def unpack_weight(words, scales, fmt):
    g, p, n, _ = words.shape
    if fmt == "e4m3":
        vals = np.ascontiguousarray(words).view(ml_dtypes.float8_e4m3fn).astype(np.float64)
    else:
        nib = np.empty((g, p, n, 4), np.uint8)
        nib[..., 0::2] = words & 0xF
        nib[..., 1::2] = words >> 4
        vals = E2M1[nib]
    vals = vals * np.repeat(np.exp2(scales.astype(np.float64) - 127.0), 8, axis=1)[..., None]
    return vals.transpose(0, 1, 3, 2).reshape(g * 512, n)
def pack4(w):
    words, scales = pack_weight(w, "e2m1")
    return words.reshape(words.shape[0], 128, -1), scales


def unpack4(words, scales):
    return unpack_weight(words.reshape(words.shape[0], 128, -1, 2), scales, "e2m1")


B, S, D1, D2, C1, C2 = 2, 1024, 512, 1024, 1024, 512


def leaky(z):
    return np.where(z > 0, z, 0.2 * z)


def draw0():
    s1, s2 = mx_kscale(D1), mx_kscale(D2)
    u = mx_kscale(S)
    x1 = np.random.standard_normal((B, S, D1)) * s1
    x2 = np.random.standard_normal((B, S, D2)) * s2 / u[:, None]
    w1 = np.random.standard_normal((D1, C1)) * (1.4 / np.sqrt(D1)) / s1[:, None]
    w2 = np.random.standard_normal((D2, C2)) * (1.4 / np.sqrt(D2)) / s2[:, None]
    m = np.random.standard_normal((B, S)) * u
    a = np.random.standard_normal((B, C1, C2)) * 0.5
    w1_words, w1_scales = pack4(w1)
    w2_words, w2_scales = pack4(w2)
    return {"x1": bf(x1), "x2": bf(x2), "w1_words": w1_words, "w1_scales": w1_scales, "w2_words": w2_words, "w2_scales": w2_scales, "m": bf(m), "a": bf(a)}


def core(x1, x2, w1_words, w1_scales, w2_words, w2_scales, m, a):
    z1 = mxq(f64(x1), 2, "e4m3") @ unpack4(w1_words, w1_scales)
    z2 = mxq(f64(x2), 2, "e4m3") @ unpack4(w2_words, w2_scales)
    f1 = leaky(z1)
    f2 = leaky(z2)
    fm = f1 * f64(m)[:, :, None]
    gram = (mxq(fm, 1, "e4m3").transpose(0, 2, 1) @ mxq(f2, 1, "e4m3")) / np.sqrt(S)
    return np.tanh(gram - f64(a))


def e4m3fn_bytes(y):
    return np.clip(np.asarray(y, np.float64), -448.0, 448.0).astype(np.float32).astype(ml_dtypes.float8_e4m3fn).view(np.uint8)


def e4m3fn_values(b):
    return np.asarray(b, np.uint8).view(ml_dtypes.float8_e4m3fn).astype(np.float64)


def setup_inputs():
    d = draw0()
    x0 = np.asarray(d['x1']).astype(np.float64)
    s = (np.max(np.abs(x0), axis=(0, 1), keepdims=True) / 448.0).astype(np.float32)
    out = {}
    for k, v in d.items():
        if k == 'x1':
            out['x1_bytes'] = e4m3fn_bytes(x0 / s.astype(np.float64))
            out['x1_scale'] = s
        else:
            out[k] = v
    return out


def reference(x1_bytes, x1_scale, x2, w1_words, w1_scales, w2_words, w2_scales, m, a):
    return core(e4m3fn_values(x1_bytes) * x1_scale.astype(np.float64), x2, w1_words, w1_scales, w2_words, w2_scales, m, a)

@@ -1,0 +1,298 @@
+from contextlib import ExitStack
+
+import concourse.mybir as mybir
+from concourse.masks import make_identity
+
+F32 = mybir.dt.float32
+BF16 = mybir.dt.bfloat16
+U32 = mybir.dt.uint32
+I32 = mybir.dt.int32
+U8 = mybir.dt.uint8
+FP8 = mybir.dt.float8_e4m3fn
+FP8X4 = mybir.dt.float8_e4m3fn_x4
+FP4X4 = mybir.dt.float4_e2m1fn_x4
+ALU = mybir.AluOpType
+ACT = mybir.ActivationFunctionType
+
+B, S, D1, D2, C1, C2 = 2, 1024, 512, 1024, 1024, 512
+P = 128
+FLOPS = 2 * B * S * (D1 * C1 + D2 * C2 + C1 * C2)
+UNITS = 4
+SLOPE = 0.2
+SIGN_ON_SCALAR = (0, 1)
+
+
+def tile_crosslayerguidedstylegramlogcoshgrad_w4_kernel(
+    tc, x1_bytes, x1_scale, x2, w1_words, w1_scales, w2_words, w2_scales, m, a, out
+):
+    nc = tc.nc
+    with ExitStack() as ctx:
+        keep = ctx.enter_context(tc.tile_pool(name="keep", bufs=1))
+        xp = ctx.enter_context(tc.tile_pool(name="xp", bufs=4))
+        wp = ctx.enter_context(tc.tile_pool(name="wp", bufs=3))
+        yp = ctx.enter_context(tc.tile_pool(name="yp", bufs=3))
+        fp = ctx.enter_context(tc.tile_pool(name="fp", bufs=3))
+        ep = ctx.enter_context(tc.tile_pool(name="ep", bufs=4))
+        ps_t = ctx.enter_context(tc.psum_pool(name="ps_t", bufs=2))
+        ps_z = ctx.enter_context(tc.psum_pool(name="ps_z", bufs=4))
+        ps_g = ctx.enter_context(tc.psum_pool(name="ps_g", bufs=2))
+
+        ident = keep.tile([P, P], F32, name="ident")
+        make_identity(nc, ident[:])
+
+        ctx.enter_context(tc.manual_schedule())
+
+        sc = keep.tile([P, D1], F32, name="sc")
+        nc.scalar.dma_start(out=sc[:], in_=x1_scale.rearrange("o q k -> (o q k)").partition_broadcast(P))
+
+        warm = keep.tile([P, 1], F32, name="warm")
+        nc.vector.memset(warm[:], 0.0)
+        nc.scalar.activation(out=warm[:], in_=warm[:], func=ACT.Tanh)
+
+        w1c = keep.tile([P, 2 * C1], U8, name="w1c", align_bytes=256)
+        w2c = keep.tile([P, 2, 2 * C2], U8, name="w2c", align_bytes=256)
+        ws = keep.tile([P, 2048], U8, name="ws", align_bytes=256)
+        nc.vector.memset(ws[:].bitcast(I32), 0)
+        w1s = ws[:, 0:C1]
+        m_sb = keep.tile([P, UNITS, 4], BF16, name="m_sb")
+        a_sb = [keep.tile([P, 8, C2], BF16, name="a_sb%d" % b) for b in range(B)]
+
+        x1b = [xp.tile([P, 4, D1], U8, name="x1b") for u in range(UNITS)]
+        x2b = [xp.tile([P, 4, D2], BF16, name="x2b") for u in range(UNITS)]
+
+        def load_x1(u):
+            rows = x1_bytes[u // 2, 512 * (u % 2) : 512 * (u % 2) + 512, :]
+            nc.sync.dma_start(out=x1b[u][:], in_=rows.rearrange("(p t) k -> p t k", t=4))
+
+        def load_x2(u, t0, t1):
+            rows = x2[u // 2, 512 * (u % 2) : 512 * (u % 2) + 512, :].rearrange("(p t) k -> p t k", t=4)
+            nc.sync.dma_start(out=x2b[u][:, t0:t1, :], in_=rows[:, t0:t1, :])
+
+        load_x1(0)
+        load_x2(0, 0, 2)
+        load_x2(0, 2, 4)
+        nc.sync.dma_start(
+            out=m_sb[:], in_=m.rearrange("b (g p t) -> p (b g) t", p=P, t=4)
+        )
+        nc.sync.dma_start(
+            out=w2c[:].bitcast(I32), in_=w2_words.rearrange("g p n -> p g n").bitcast(I32)
+        )
+        for q in range(4):
+            nc.sync.dma_start(
+                out=ws[32 * q : 32 * q + 4, 1024:2048].rearrange("p (g n) -> p g n", g=2).bitcast(I32),
+                in_=w2_scales[:, 4 * q : 4 * q + 4, :].rearrange("g q n -> q g n").bitcast(I32),
+            )
+        for q in range(4):
+            nc.sync.dma_start(
+                out=ws[32 * q : 32 * q + 4, 0:1024].bitcast(I32),
+                in_=w1_scales[0, 4 * q : 4 * q + 4, :].bitcast(I32),
+            )
+        nc.sync.dma_start(out=w1c[:].bitcast(I32), in_=w1_words[0].bitcast(I32))
+        for u in range(1, UNITS):
+            load_x1(u)
+            load_x2(u, 0, 4)
+            if u >= 2:
+                b = u - 2
+                nc.sync.dma_start(out=a_sb[b][:], in_=a[b].rearrange("(i p) n -> p i n", p=P))
+
+        sgn = keep.tile([P, UNITS, 4], F32, name="sgn")
+        mag = keep.tile([P, UNITS, 4], F32, name="mag")
+        sgnb = keep.tile([P, UNITS, 4], BF16, name="sgnb")
+
+        x1w = [None] * UNITS
+        x1g = [None] * UNITS
+        x2g = [None] * UNITS
+        x1q = [None] * UNITS
+        x2q = [None] * UNITS
+        ys = {}
+        fs = {}
+        fq = {}
+        es = {}
+
+        def widen(u):
+            w = wp.tile([P, 4, D1], BF16, name="x1w", align_bytes=64)
+            for t in range(4):
+                nc.vector.tensor_tensor(out=w[:, t, :], in0=x1b[u][:, t, :].bitcast(FP8), in1=sc[:], op=ALU.mult)
+            x1w[u] = w
+
+        def turn_x2(u):
+            g = wp.tile([P, 4, 2, P, 4], BF16, name="x2g", align_bytes=64)
+            x2g[u] = g
+            for t in range(4):
+                words = x2b[u][:, t, :].bitcast(F32)
+                tr = ps_t.tile([P, 4, P], F32, name="tr")
+                for j in range(4):
+                    k0 = 256 * (j // 2) + j % 2
+                    nc.tensor.transpose(tr[:, j, :], words[:, k0 : 256 * (j // 2) + 256 : 2], ident[:])
+                nc.scalar.copy(out=g[:, t].bitcast(F32), in_=tr[:].rearrange("p (g e) m -> p g m e", e=2))
+
+        def turn_x1(u):
+            g = wp.tile([P, 4, P, 4], BF16, name="x1g", align_bytes=64)
+            x1g[u] = g
+            for h in range(2):
+                tr = ps_t.tile([P, 4, P], F32, name="tr")
+                for j in range(4):
+                    words = x1w[u][:, 2 * h + j // 2, :].bitcast(F32)
+                    nc.tensor.transpose(tr[:, j, :], words[:, j % 2 : 256 : 2], ident[:])
+                nc.scalar.copy(
+                    out=g[:, 2 * h : 2 * h + 2].bitcast(F32), in_=tr[:].rearrange("p (t e) m -> p t m e", e=2)
+                )
+
+        def quant(src, name, n):
+            c = fp.tile([P, n // 4], U32, name=name + "c", align_bytes=256)
+            s = fp.tile([P, n // 4], U8, name=name + "s", align_bytes=256)
+            for i in range(0, n, 2048):
+                nc.vector.quantize_mx(
+                    out=c[:, i // 4 : i // 4 + 512].bitcast(FP8X4),
+                    scales=s[:, i // 4 : i // 4 + 512],
+                    in_=src[:, i : i + 2048],
+                )
+            return c, s
+
+        def quant_x2(u):
+            x2q[u] = quant(x2g[u][:].rearrange("p t g m k -> p (t g m k)"), "x2", 4096)
+
+        def quant_x1(u):
+            x1q[u] = quant(x1g[u][:].rearrange("p t m k -> p (t m k)"), "x1", 2048)
+
+        def mm(o, lq, lc, rw, rs, start, stop):
+            nc.tensor.matmul_mx(
+                out=o,
+                lhsT=lq[0][:, lc : lc + P].bitcast(FP8X4),
+                lhsT_scale=lq[1][:, lc : lc + P],
+                rhs=rw,
+                rhs_scale=rs,
+                start=start,
+                stop=stop,
+            )
+
+        def z2(u):
+            y = yp.tile([P, 4, C2], F32, name="y")
+            ys[u, 2] = y
+            for t in range(4):
+                z = ps_z.tile([P, 512], F32, name="z")
+                for g in range(2):
+                    mm(z[:], x2q[u], (2 * t + g) * P, w2c[:, g, :].bitcast(FP4X4),
+                       ws[:, 1024 + 512 * g : 1536 + 512 * g], g == 0, g == 1)
+                if u in SIGN_ON_SCALAR:
+                    if t == 0:
+                        v = yp.tile([P, 4, C2], BF16, name="v")
+                        ys[u, 3] = v
+                    nc.scalar.activation(out=v[:, t, :], in_=z[:], func=ACT.Sign)
+                    nc.scalar.activation(out=y[:, t, :], in_=z[:], func=ACT.Copy, scale=sgn[:, u, t : t + 1])
+                else:
+                    nc.scalar.copy(out=y[:, t, :], in_=z[:])
+
+        def z1(u, h):
+            y = yp.tile([P, 4, C2], F32, name="y")
+            ys[u, h] = y
+            for t in range(4):
+                z = ps_z.tile([P, 512], F32, name="z")
+                mm(z[:], x1q[u], t * P, w1c[:, 1024 * h : 1024 * h + 1024].bitcast(FP4X4),
+                   ws[:, 512 * h : 512 * h + 512], True, True)
+                nc.scalar.activation(out=y[:, t, :], in_=z[:], func=ACT.Copy, scale=mag[:, u, t : t + 1])
+
+        def leaky(u, k):
+            y = ys[u, k][:].rearrange("p t c -> p c t")
+            f = fp.tile([P, 512, 4], BF16, name="f", align_bytes=64)
+            fs[u, k] = f
+            if k == 2 and u in SIGN_ON_SCALAR:
+                v = ys[u, 3][:].rearrange("p t c -> p c t")
+                nc.vector.scalar_tensor_tensor(out=f[:], in0=v, scalar=SLOPE, in1=y, op0=ALU.max, op1=ALU.mult)
+            else:
+                nc.vector.scalar_tensor_tensor(out=f[:], in0=y, scalar=SLOPE, in1=y, op0=ALU.mult, op1=ALU.max)
+
+        def flip(u):
+            if u not in SIGN_ON_SCALAR:
+                f = fs[u, 2]
+                s4 = sgnb[:, u, :].unsqueeze(1).to_broadcast([P, 512, 4])
+                nc.vector.tensor_tensor(out=f[:], in0=f[:], in1=s4, op=ALU.mult)
+
+        def quant_f(u, k):
+            c = keep.tile([P, 512], U32, name="fc%d_%d" % (u, k), align_bytes=256)
+            s = keep.tile([P, 512], U8, name="fs%d_%d" % (u, k), align_bytes=256)
+            nc.vector.quantize_mx(
+                out=c[:].bitcast(FP8X4), scales=s[:], in_=fs[u, k][:].rearrange("p c t -> p (c t)")
+            )
+            fq[u, k] = (c, s)
+
+        def gram(b, i):
+            g = ps_g.tile([P, C2], F32, name="g")
+            for n in range(2):
+                u = 2 * b + n
+                mm(g[:], fq[u, i // 4], (i % 4) * P, fq[u, 2][0][:].bitcast(FP8X4), fq[u, 2][1][:], n == 0, n == 1)
+            e = ep.tile([P, C2], F32, name="e")
+            es[b, i] = e
+            nc.vector.scalar_tensor_tensor(
+                out=e[:], in0=g[:], scalar=1.0 / 32.0, in1=a_sb[b][:, i, :], op0=ALU.mult, op1=ALU.subtract
+            )
+
+        def finish(b, i):
+            e = es[b, i]
+            o = ep.tile([P, C2], F32, name="o")
+            nc.scalar.activation(out=o[:], in_=e[:], func=ACT.Tanh)
+            nc.sync.dma_start(out=out[b, P * i : P * i + P, :], in_=o[:])
+
+        widen(0)
+        turn_x2(0)
+        quant_x2(0)
+        nc.vector.tensor_scalar(out=sgn[:], in0=m_sb[:], scalar1=0.0, scalar2=2.0, op0=ALU.is_ge, op1=ALU.mult)
+        nc.vector.tensor_scalar(out=sgn[:], in0=sgn[:], scalar1=-1.0, scalar2=None, op0=ALU.add)
+        nc.vector.tensor_tensor(out=mag[:], in0=m_sb[:], in1=sgn[:], op=ALU.mult)
+        nc.vector.tensor_copy(out=sgnb[:], in_=sgn[:])
+        turn_x1(0)
+        quant_x1(0)
+        widen(1)
+        z2(0)
+
+        todo = []
+
+        def next_gram():
+            if todo:
+                gram(*todo[0])
+
+        def next_finish():
+            if todo:
+                finish(*todo[0])
+                todo.remove(todo[0])
+
+        for u in range(UNITS):
+            more = u + 1 < UNITS
+            z1(u, 0)
+            leaky(u, 2)
+            next_gram()
+            if more:
+                turn_x2(u + 1)
+            next_finish()
+            leaky(u, 0)
+            if more:
+                quant_x2(u + 1)
+            z1(u, 1)
+            flip(u)
+            next_gram()
+            leaky(u, 1)
+            quant_f(u, 2)
+            next_finish()
+            if more:
+                turn_x1(u + 1)
+                quant_x1(u + 1)
+            quant_f(u, 0)
+            next_gram()
+            if more:
+                z2(u + 1)
+            next_finish()
+            if u + 2 < UNITS:
+                widen(u + 2)
+            next_gram()
+            quant_f(u, 1)
+            next_finish()
+            if u % 2 == 1:
+                todo.extend([(u // 2, i) for i in range(8)])
+        for i in range(4):
+            gram(1, i)
+            if i > 0:
+                finish(1, i - 1)
+        for i in range(4, 8):
+            gram(1, i)
+            finish(1, i - 1)
+        finish(1, 7)

@@ -19,7 +19,7 @@ P = 128
 FLOPS = 2 * B * S * (D1 * C1 + D2 * C2 + C1 * C2)
 UNITS = 4
 SLOPE = 0.2
-SIGN_ON_SCALAR = (0, 1)
+TWICE = ()
 
 
 def tile_crosslayerguidedstylegramlogcoshgrad_w4_kernel(
@@ -32,7 +32,7 @@ def tile_crosslayerguidedstylegramlogcoshgrad_w4_kernel(
         wp = ctx.enter_context(tc.tile_pool(name="wp", bufs=3))
         yp = ctx.enter_context(tc.tile_pool(name="yp", bufs=3))
         fp = ctx.enter_context(tc.tile_pool(name="fp", bufs=3))
-        ep = ctx.enter_context(tc.tile_pool(name="ep", bufs=4))
+        ep = ctx.enter_context(tc.tile_pool(name="ep", bufs=8))
         ps_t = ctx.enter_context(tc.psum_pool(name="ps_t", bufs=2))
         ps_z = ctx.enter_context(tc.psum_pool(name="ps_z", bufs=4))
         ps_g = ctx.enter_context(tc.psum_pool(name="ps_g", bufs=2))
@@ -97,6 +97,7 @@ def tile_crosslayerguidedstylegramlogcoshgrad_w4_kernel(
 
         sgn = keep.tile([P, UNITS, 4], F32, name="sgn")
         mag = keep.tile([P, UNITS, 4], F32, name="mag")
+        mag5 = keep.tile([P, UNITS, 4], F32, name="mag5")
         sgnb = keep.tile([P, UNITS, 4], BF16, name="sgnb")
 
         x1w = [None] * UNITS
@@ -167,46 +168,46 @@ def tile_crosslayerguidedstylegramlogcoshgrad_w4_kernel(
             )
 
         def z2(u):
-            y = yp.tile([P, 4, C2], F32, name="y")
+            y = yp.tile([P, C2, 4], F32, name="y")
             ys[u, 2] = y
-            for t in range(4):
-                z = ps_z.tile([P, 512], F32, name="z")
-                for g in range(2):
-                    mm(z[:], x2q[u], (2 * t + g) * P, w2c[:, g, :].bitcast(FP4X4),
-                       ws[:, 1024 + 512 * g : 1536 + 512 * g], g == 0, g == 1)
-                if u in SIGN_ON_SCALAR:
-                    if t == 0:
-                        v = yp.tile([P, 4, C2], BF16, name="v")
-                        ys[u, 3] = v
-                    nc.scalar.activation(out=v[:, t, :], in_=z[:], func=ACT.Sign)
-                    nc.scalar.activation(out=y[:, t, :], in_=z[:], func=ACT.Copy, scale=sgn[:, u, t : t + 1])
-                else:
-                    nc.scalar.copy(out=y[:, t, :], in_=z[:])
+            for q in range(4):
+                z = ps_z.tile([P, 4, P], F32, name="z")
+                for t in range(4):
+                    for g in range(2):
+                        mm(z[:, t, :], x2q[u], (2 * t + g) * P, w2c[:, g, 256 * q : 256 * q + 256].bitcast(FP4X4),
+                           ws[:, 1024 + 512 * g + P * q : 1024 + 512 * g + P * q + P], g == 0, g == 1)
+                nc.scalar.copy(out=y[:, P * q : P * q + P, :], in_=z[:].rearrange("p t c -> p c t"))
 
         def z1(u, h):
             y = yp.tile([P, 4, C2], F32, name="y")
             ys[u, h] = y
+            if (u, h) in TWICE:
+                v = yp.tile([P, 4, C2], F32, name="v")
+                ys[u, h + 3] = v
             for t in range(4):
                 z = ps_z.tile([P, 512], F32, name="z")
                 mm(z[:], x1q[u], t * P, w1c[:, 1024 * h : 1024 * h + 1024].bitcast(FP4X4),
                    ws[:, 512 * h : 512 * h + 512], True, True)
                 nc.scalar.activation(out=y[:, t, :], in_=z[:], func=ACT.Copy, scale=mag[:, u, t : t + 1])
+                if (u, h) in TWICE:
+                    nc.scalar.activation(out=v[:, t, :], in_=z[:], func=ACT.Copy, scale=mag5[:, u, t : t + 1])
 
         def leaky(u, k):
-            y = ys[u, k][:].rearrange("p t c -> p c t")
             f = fp.tile([P, 512, 4], BF16, name="f", align_bytes=64)
             fs[u, k] = f
-            if k == 2 and u in SIGN_ON_SCALAR:
-                v = ys[u, 3][:].rearrange("p t c -> p c t")
-                nc.vector.scalar_tensor_tensor(out=f[:], in0=v, scalar=SLOPE, in1=y, op0=ALU.max, op1=ALU.mult)
-            else:
-                nc.vector.scalar_tensor_tensor(out=f[:], in0=y, scalar=SLOPE, in1=y, op0=ALU.mult, op1=ALU.max)
+            if (u, k) in TWICE:
+                a0 = ys[u, k][:].rearrange("p t (c i) -> p c t i", i=2)
+                a1 = ys[u, k + 3][:].rearrange("p t (c i) -> p c t i", i=2)
+                nc.vector.tensor_tensor(
+                    out=f[:].rearrange("p (c i) t -> p c t i", i=2), in0=a0, in1=a1, op=ALU.max)
+                return
+            y = ys[u, k][:] if k == 2 else ys[u, k][:].rearrange("p t c -> p c t")
+            nc.vector.scalar_tensor_tensor(out=f[:], in0=y, scalar=SLOPE, in1=y, op0=ALU.mult, op1=ALU.max)
 
         def flip(u):
-            if u not in SIGN_ON_SCALAR:
-                f = fs[u, 2]
-                s4 = sgnb[:, u, :].unsqueeze(1).to_broadcast([P, 512, 4])
-                nc.vector.tensor_tensor(out=f[:], in0=f[:], in1=s4, op=ALU.mult)
+            f = fs[u, 2]
+            s4 = sgnb[:, u, :].unsqueeze(1).to_broadcast([P, 512, 4])
+            nc.vector.tensor_tensor(out=f[:], in0=f[:], in1=s4, op=ALU.mult)
 
         def quant_f(u, k):
             c = keep.tile([P, 512], U32, name="fc%d_%d" % (u, k), align_bytes=256)
@@ -217,7 +218,7 @@ def tile_crosslayerguidedstylegramlogcoshgrad_w4_kernel(
             fq[u, k] = (c, s)
 
         def gram(b, i):
-            g = ps_g.tile([P, C2], F32, name="g")
+            g = ps_z.tile([P, C2], F32, name="z") if b == 1 else ps_g.tile([P, C2], F32, name="g")
             for n in range(2):
                 u = 2 * b + n
                 mm(g[:], fq[u, i // 4], (i % 4) * P, fq[u, 2][0][:].bitcast(FP8X4), fq[u, 2][1][:], n == 0, n == 1)
@@ -229,9 +230,8 @@ def tile_crosslayerguidedstylegramlogcoshgrad_w4_kernel(
 
         def finish(b, i):
             e = es[b, i]
-            o = ep.tile([P, C2], F32, name="o")
-            nc.scalar.activation(out=o[:], in_=e[:], func=ACT.Tanh)
-            nc.sync.dma_start(out=out[b, P * i : P * i + P, :], in_=o[:])
+            nc.scalar.activation(out=e[:], in_=e[:], func=ACT.Tanh)
+            nc.sync.dma_start(out=out[b, P * i : P * i + P, :], in_=e[:])
 
         widen(0)
         turn_x2(0)
@@ -240,6 +240,7 @@ def tile_crosslayerguidedstylegramlogcoshgrad_w4_kernel(
         nc.vector.tensor_scalar(out=sgn[:], in0=sgn[:], scalar1=-1.0, scalar2=None, op0=ALU.add)
         nc.vector.tensor_tensor(out=mag[:], in0=m_sb[:], in1=sgn[:], op=ALU.mult)
         nc.vector.tensor_copy(out=sgnb[:], in_=sgn[:])
+        nc.vector.tensor_scalar(out=mag5[:], in0=mag[:], scalar1=SLOPE, scalar2=None, op0=ALU.mult)
         turn_x1(0)
         quant_x1(0)
         widen(1)

@@ -15,11 +15,14 @@ ALU = mybir.AluOpType
 ACT = mybir.ActivationFunctionType
 
 B, S, D1, D2, C1, C2 = 2, 1024, 512, 1024, 1024, 512
-P = 128
 FLOPS = 2 * B * S * (D1 * C1 + D2 * C2 + C1 * C2)
-UNITS = 4
+P = 128
+T = 4
+K_PASS = P * T
+N = 512
+UNITS = B * S // K_PASS
 SLOPE = 0.2
-TWICE = ()
+EPILOGUE = {2: (0, 1, 0, 1, 0), 3: (2, 0, 2, 1, 1)}
 
 
 def tile_crosslayerguidedstylegramlogcoshgrad_w4_kernel(
@@ -28,272 +31,312 @@ def tile_crosslayerguidedstylegramlogcoshgrad_w4_kernel(
     nc = tc.nc
     with ExitStack() as ctx:
         keep = ctx.enter_context(tc.tile_pool(name="keep", bufs=1))
-        xp = ctx.enter_context(tc.tile_pool(name="xp", bufs=4))
-        wp = ctx.enter_context(tc.tile_pool(name="wp", bufs=3))
+        xp = ctx.enter_context(tc.tile_pool(name="xp", bufs=UNITS))
+        wp = ctx.enter_context(tc.tile_pool(name="wp", bufs=2))
         yp = ctx.enter_context(tc.tile_pool(name="yp", bufs=3))
+        up = ctx.enter_context(tc.tile_pool(name="up", bufs=2))
         fp = ctx.enter_context(tc.tile_pool(name="fp", bufs=3))
         ep = ctx.enter_context(tc.tile_pool(name="ep", bufs=8))
         ps_t = ctx.enter_context(tc.psum_pool(name="ps_t", bufs=2))
         ps_z = ctx.enter_context(tc.psum_pool(name="ps_z", bufs=4))
         ps_g = ctx.enter_context(tc.psum_pool(name="ps_g", bufs=2))
 
+        zb = keep.tile([P, N], BF16, name="zb")
+        nc.gpsimd.memset(zb[:], 0.0)
         ident = keep.tile([P, P], F32, name="ident")
         make_identity(nc, ident[:])
 
         ctx.enter_context(tc.manual_schedule())
 
-        sc = keep.tile([P, D1], F32, name="sc")
-        nc.scalar.dma_start(out=sc[:], in_=x1_scale.rearrange("o q k -> (o q k)").partition_broadcast(P))
-
+        sct = keep.tile([P, T], F32, name="sct")
+        nc.scalar.dma_start(out=sct[:], in_=x1_scale.rearrange("o q (p j) -> p (o q j)", j=T))
         warm = keep.tile([P, 1], F32, name="warm")
         nc.vector.memset(warm[:], 0.0)
         nc.scalar.activation(out=warm[:], in_=warm[:], func=ACT.Tanh)
 
         w1c = keep.tile([P, 2 * C1], U8, name="w1c", align_bytes=256)
         w2c = keep.tile([P, 2, 2 * C2], U8, name="w2c", align_bytes=256)
-        ws = keep.tile([P, 2048], U8, name="ws", align_bytes=256)
+        ws = keep.tile([P, C1 + 2 * C2], U8, name="ws", align_bytes=256)
         nc.vector.memset(ws[:].bitcast(I32), 0)
-        w1s = ws[:, 0:C1]
-        m_sb = keep.tile([P, UNITS, 4], BF16, name="m_sb")
-        a_sb = [keep.tile([P, 8, C2], BF16, name="a_sb%d" % b) for b in range(B)]
+        m_sb = keep.tile([P, UNITS, T], BF16, name="m_sb")
+        a_sb = [keep.tile([P, 2, T, C2], BF16, name="a_sb%d" % b) for b in range(B)]
+        x1b = [xp.tile([P, T, D1], U8, name="x1b") for u in range(UNITS)]
+        x2b = [xp.tile([P, T, D2], BF16, name="x2b") for u in range(UNITS)]
 
-        x1b = [xp.tile([P, 4, D1], U8, name="x1b") for u in range(UNITS)]
-        x2b = [xp.tile([P, 4, D2], BF16, name="x2b") for u in range(UNITS)]
+        def unit_rows(x, u):
+            return x[u // 2, K_PASS * (u % 2) : K_PASS * (u % 2) + K_PASS, :].rearrange("(p t) k -> p t k", t=T)
 
         def load_x1(u):
-            rows = x1_bytes[u // 2, 512 * (u % 2) : 512 * (u % 2) + 512, :]
-            nc.sync.dma_start(out=x1b[u][:], in_=rows.rearrange("(p t) k -> p t k", t=4))
+            nc.sync.dma_start(out=x1b[u][:], in_=unit_rows(x1_bytes, u))
 
         def load_x2(u, t0, t1):
-            rows = x2[u // 2, 512 * (u % 2) : 512 * (u % 2) + 512, :].rearrange("(p t) k -> p t k", t=4)
-            nc.sync.dma_start(out=x2b[u][:, t0:t1, :], in_=rows[:, t0:t1, :])
+            nc.sync.dma_start(out=x2b[u][:, t0:t1, :], in_=unit_rows(x2, u)[:, t0:t1, :])
 
         load_x1(0)
         load_x2(0, 0, 2)
         load_x2(0, 2, 4)
-        nc.sync.dma_start(
-            out=m_sb[:], in_=m.rearrange("b (g p t) -> p (b g) t", p=P, t=4)
-        )
-        nc.sync.dma_start(
-            out=w2c[:].bitcast(I32), in_=w2_words.rearrange("g p n -> p g n").bitcast(I32)
-        )
+        nc.sync.dma_start(out=m_sb[:], in_=m.rearrange("b (g p t) -> p (b g) t", p=P, t=T))
+        nc.sync.dma_start(out=w2c[:].bitcast(I32), in_=w2_words.rearrange("g p n -> p g n").bitcast(I32))
         for q in range(4):
             nc.sync.dma_start(
-                out=ws[32 * q : 32 * q + 4, 1024:2048].rearrange("p (g n) -> p g n", g=2).bitcast(I32),
+                out=ws[32 * q : 32 * q + 4, C1:].rearrange("p (g n) -> p g n", g=2).bitcast(I32),
                 in_=w2_scales[:, 4 * q : 4 * q + 4, :].rearrange("g q n -> q g n").bitcast(I32),
             )
         for q in range(4):
             nc.sync.dma_start(
-                out=ws[32 * q : 32 * q + 4, 0:1024].bitcast(I32),
-                in_=w1_scales[0, 4 * q : 4 * q + 4, :].bitcast(I32),
+                out=ws[32 * q : 32 * q + 4, 0:C1].bitcast(I32), in_=w1_scales[0, 4 * q : 4 * q + 4, :].bitcast(I32)
             )
         nc.sync.dma_start(out=w1c[:].bitcast(I32), in_=w1_words[0].bitcast(I32))
         for u in range(1, UNITS):
             load_x1(u)
             load_x2(u, 0, 4)
             if u >= 2:
-                b = u - 2
-                nc.sync.dma_start(out=a_sb[b][:], in_=a[b].rearrange("(i p) n -> p i n", p=P))
+                nc.sync.dma_start(out=a_sb[u - 2][:], in_=a[u - 2].rearrange("(h p i) n -> p h i n", p=P, i=T))
 
-        sgn = keep.tile([P, UNITS, 4], F32, name="sgn")
-        mag = keep.tile([P, UNITS, 4], F32, name="mag")
-        mag5 = keep.tile([P, UNITS, 4], F32, name="mag5")
-        sgnb = keep.tile([P, UNITS, 4], BF16, name="sgnb")
+        sc = keep.tile([P, P, T], F32, name="sc")
+        sgn = keep.tile([P, UNITS, T], F32, name="sgn")
+        mag = keep.tile([P, UNITS, T], F32, name="mag")
+        sgnb = keep.tile([P, UNITS, T], BF16, name="sgnb")
+        x1w, x1g, x2g, x1q, x2q, y, uu, f, fq, e = {}, {}, {}, {}, {}, {}, {}, {}, {}, {}
 
-        x1w = [None] * UNITS
-        x1g = [None] * UNITS
-        x2g = [None] * UNITS
-        x1q = [None] * UNITS
-        x2q = [None] * UNITS
-        ys = {}
-        fs = {}
-        fq = {}
-        es = {}
+        def keep_warm(n):
+            for i in range(n):
+                g = ps_g.tile([P, N], F32, name="g")
+                nc.tensor.matmul(g[:], lhsT=zb[:, 0:P], rhs=zb[:], start=True, stop=True)
+
+        def spread_scales():
+            tr = ps_t.tile([P, T, P], F32, name="tr")
+            for j in range(T):
+                nc.tensor.transpose(tr[:, j, :], sct[:, j : j + 1].to_broadcast([P, P]), ident[:])
+            nc.vector.tensor_copy(out=sc[:], in_=tr[:].rearrange("p j n -> p n j"))
+
+        def split_m():
+            nc.vector.tensor_scalar(out=sgn[:], in0=m_sb[:], scalar1=0.0, scalar2=2.0, op0=ALU.is_ge, op1=ALU.mult)
+            nc.vector.tensor_scalar(out=sgn[:], in0=sgn[:], scalar1=-1.0, scalar2=None, op0=ALU.add)
+            nc.vector.tensor_tensor(out=mag[:], in0=m_sb[:], in1=sgn[:], op=ALU.mult)
+            nc.vector.tensor_copy(out=sgnb[:], in_=sgn[:])
 
         def widen(u):
-            w = wp.tile([P, 4, D1], BF16, name="x1w", align_bytes=64)
-            for t in range(4):
-                nc.vector.tensor_tensor(out=w[:, t, :], in0=x1b[u][:, t, :].bitcast(FP8), in1=sc[:], op=ALU.mult)
+            w = wp.tile([P, T, D1], BF16, name="x1w", align_bytes=64)
             x1w[u] = w
-
-        def turn_x2(u):
-            g = wp.tile([P, 4, 2, P, 4], BF16, name="x2g", align_bytes=64)
-            x2g[u] = g
-            for t in range(4):
-                words = x2b[u][:, t, :].bitcast(F32)
-                tr = ps_t.tile([P, 4, P], F32, name="tr")
-                for j in range(4):
-                    k0 = 256 * (j // 2) + j % 2
-                    nc.tensor.transpose(tr[:, j, :], words[:, k0 : 256 * (j // 2) + 256 : 2], ident[:])
-                nc.scalar.copy(out=g[:, t].bitcast(F32), in_=tr[:].rearrange("p (g e) m -> p g m e", e=2))
-
-        def turn_x1(u):
-            g = wp.tile([P, 4, P, 4], BF16, name="x1g", align_bytes=64)
-            x1g[u] = g
-            for h in range(2):
-                tr = ps_t.tile([P, 4, P], F32, name="tr")
-                for j in range(4):
-                    words = x1w[u][:, 2 * h + j // 2, :].bitcast(F32)
-                    nc.tensor.transpose(tr[:, j, :], words[:, j % 2 : 256 : 2], ident[:])
-                nc.scalar.copy(
-                    out=g[:, 2 * h : 2 * h + 2].bitcast(F32), in_=tr[:].rearrange("p (t e) m -> p t m e", e=2)
+            for t in range(T):
+                nc.vector.tensor_tensor(
+                    out=w[:, t, :], in0=x1b[u][:, t, :].bitcast(FP8), in1=sc[:].rearrange("p n j -> p (n j)"), op=ALU.mult
                 )
 
-        def quant(src, name, n):
-            c = fp.tile([P, n // 4], U32, name=name + "c", align_bytes=256)
-            s = fp.tile([P, n // 4], U8, name=name + "s", align_bytes=256)
-            for i in range(0, n, 2048):
-                nc.vector.quantize_mx(
-                    out=c[:, i // 4 : i // 4 + 512].bitcast(FP8X4),
-                    scales=s[:, i // 4 : i // 4 + 512],
-                    in_=src[:, i : i + 2048],
-                )
+        def turn_x2(u, t):
+            if t == 0:
+                x2g[u] = wp.tile([P, T, 2, P, T], BF16, name="x2g", align_bytes=64)
+            words = x2b[u][:, t, :].bitcast(F32)
+            tr = ps_t.tile([P, T, P], F32, name="tr")
+            for j in range(4):
+                k0 = 256 * (j // 2)
+                nc.tensor.transpose(tr[:, j, :], words[:, k0 + j % 2 : k0 + 256 : 2], ident[:])
+            nc.scalar.copy(out=x2g[u][:, t].bitcast(F32), in_=tr[:].rearrange("p (g e) r -> p g r e", e=2))
+
+        def turn_x1(u, h):
+            if h == 0:
+                x1g[u] = wp.tile([P, T, P, T], BF16, name="x1g", align_bytes=64)
+            tr = ps_t.tile([P, T, P], F32, name="tr")
+            for j in range(4):
+                words = x1w[u][:, 2 * h + j // 2, :].bitcast(F32)
+                nc.tensor.transpose(tr[:, j, :], words[:, j % 2 : 256 : 2], ident[:])
+            nc.scalar.copy(
+                out=x1g[u][:, 2 * h : 2 * h + 2].bitcast(F32), in_=tr[:].rearrange("p (t e) r -> p t r e", e=2)
+            )
+
+        def quantize(pool, src, names):
+            c = pool.tile([P, N], U32, name=names[0], align_bytes=256)
+            s = pool.tile([P, N], U8, name=names[1], align_bytes=256)
+            nc.vector.quantize_mx(out=c[:].bitcast(FP8X4), scales=s[:], in_=src)
             return c, s
 
-        def quant_x2(u):
-            x2q[u] = quant(x2g[u][:].rearrange("p t g m k -> p (t g m k)"), "x2", 4096)
-
-        def quant_x1(u):
-            x1q[u] = quant(x1g[u][:].rearrange("p t m k -> p (t m k)"), "x1", 2048)
-
-        def mm(o, lq, lc, rw, rs, start, stop):
-            nc.tensor.matmul_mx(
-                out=o,
-                lhsT=lq[0][:, lc : lc + P].bitcast(FP8X4),
-                lhsT_scale=lq[1][:, lc : lc + P],
-                rhs=rw,
-                rhs_scale=rs,
-                start=start,
-                stop=stop,
+        def quantize_x2(u, h):
+            x2q[u, h] = quantize(
+                fp, x2g[u][:, 2 * h : 2 * h + 2].rearrange("p t g r k -> p (t g r k)"), ("x2c%d" % h, "x2s%d" % h)
             )
 
-        def z2(u):
-            y = yp.tile([P, C2, 4], F32, name="y")
-            ys[u, 2] = y
-            for q in range(4):
-                z = ps_z.tile([P, 4, P], F32, name="z")
-                for t in range(4):
-                    for g in range(2):
-                        mm(z[:, t, :], x2q[u], (2 * t + g) * P, w2c[:, g, 256 * q : 256 * q + 256].bitcast(FP4X4),
-                           ws[:, 1024 + 512 * g + P * q : 1024 + 512 * g + P * q + P], g == 0, g == 1)
-                nc.scalar.copy(out=y[:, P * q : P * q + P, :], in_=z[:].rearrange("p t c -> p c t"))
+        def quantize_x1(u):
+            x1q[u] = quantize(fp, x1g[u][:].rearrange("p t r k -> p (t r k)"), ("x1c", "x1s"))
 
-        def z1(u, h):
-            y = yp.tile([P, 4, C2], F32, name="y")
-            ys[u, h] = y
-            if (u, h) in TWICE:
-                v = yp.tile([P, 4, C2], F32, name="v")
-                ys[u, h + 3] = v
-            for t in range(4):
-                z = ps_z.tile([P, 512], F32, name="z")
-                mm(z[:], x1q[u], t * P, w1c[:, 1024 * h : 1024 * h + 1024].bitcast(FP4X4),
-                   ws[:, 512 * h : 512 * h + 512], True, True)
-                nc.scalar.activation(out=y[:, t, :], in_=z[:], func=ACT.Copy, scale=mag[:, u, t : t + 1])
-                if (u, h) in TWICE:
-                    nc.scalar.activation(out=v[:, t, :], in_=z[:], func=ACT.Copy, scale=mag5[:, u, t : t + 1])
+        def quantize_f(u, k):
+            fq[u, k] = quantize(keep, f[u, k][:].rearrange("p c t -> p (c t)"), ("fc%d%s" % (u, k), "fs%d%s" % (u, k)))
+
+        def mx(o, left, col, words, scales, start, stop):
+            nc.tensor.matmul_mx(
+                out=o, lhsT=left[0][:, col : col + P].bitcast(FP8X4), lhsT_scale=left[1][:, col : col + P],
+                rhs=words, rhs_scale=scales, start=start, stop=stop,
+            )
+
+        def z2_plain(u, q):
+            if q == 0:
+                y[u, "2"] = yp.tile([P, N, T], F32, name="y")
+            z = ps_z.tile([P, T, P], F32, name="z")
+            for t in range(T):
+                for g in range(2):
+                    mx(z[:, t, :], x2q[u, t // 2], (2 * (t % 2) + g) * P,
+                       w2c[:, g, 2 * P * q : 2 * P * q + 2 * P].bitcast(FP4X4),
+                       ws[:, C1 + C2 * g + P * q : C1 + C2 * g + P * q + P], g == 0, g == 1)
+            nc.scalar.copy(out=y[u, "2"][:, P * q : P * q + P, :], in_=z[:].rearrange("p t c -> p c t"))
+
+        def z2_signed(u, t):
+            if t == 0:
+                y[u, "2"] = yp.tile([P, P, T, 4], F32, name="y")
+                uu[u] = up.tile([P, P, T, 4], F32, name="v")
+            z = ps_z.tile([P, N], F32, name="z")
+            for g in range(2):
+                mx(z[:], x2q[u, t // 2], (2 * (t % 2) + g) * P, w2c[:, g, :].bitcast(FP4X4),
+                   ws[:, C1 + C2 * g : C1 + C2 * g + C2], g == 0, g == 1)
+            zv = z[:].rearrange("p (c i) -> p c i", i=4)
+            nc.scalar.activation(out=uu[u][:, :, t, :], in_=zv, func=ACT.Sign)
+            nc.scalar.activation(out=y[u, "2"][:, :, t, :], in_=zv, func=ACT.Copy, scale=sgn[:, u, t : t + 1])
+
+        def z1(u, h, t):
+            if t == 0:
+                y[u, h] = yp.tile([P, P, T, 4], F32, name="y")
+            z = ps_z.tile([P, N], F32, name="z")
+            mx(z[:], x1q[u], t * P, w1c[:, 2 * N * h : 2 * N * h + 2 * N].bitcast(FP4X4), ws[:, N * h : N * h + N],
+               True, True)
+            nc.scalar.activation(
+                out=y[u, h][:, :, t, :], in_=z[:].rearrange("p (c i) -> p c i", i=4), func=ACT.Copy,
+                scale=mag[:, u, t : t + 1],
+            )
+
+        def new_f(u, k):
+            f[u, k] = fp.tile([P, N, T], BF16, name="f", align_bytes=64)
+            return f[u, k][:].rearrange("p c t -> p (c t)").rearrange("p (i n) -> p n i", i=4)
 
         def leaky(u, k):
-            f = fp.tile([P, 512, 4], BF16, name="f", align_bytes=64)
-            fs[u, k] = f
-            if (u, k) in TWICE:
-                a0 = ys[u, k][:].rearrange("p t (c i) -> p c t i", i=2)
-                a1 = ys[u, k + 3][:].rearrange("p t (c i) -> p c t i", i=2)
-                nc.vector.tensor_tensor(
-                    out=f[:].rearrange("p (c i) t -> p c t i", i=2), in0=a0, in1=a1, op=ALU.max)
-                return
-            y = ys[u, k][:] if k == 2 else ys[u, k][:].rearrange("p t c -> p c t")
-            nc.vector.scalar_tensor_tensor(out=f[:], in0=y, scalar=SLOPE, in1=y, op0=ALU.mult, op1=ALU.max)
+            o = new_f(u, k)
+            v = y[u, k][:].rearrange("p c t i -> p (c t) i")
+            if k == "2":
+                s = uu[u][:].rearrange("p c t i -> p (c t) i")
+                nc.vector.scalar_tensor_tensor(out=o, in0=s, scalar=SLOPE, in1=v, op0=ALU.max, op1=ALU.mult)
+            else:
+                nc.vector.scalar_tensor_tensor(out=o, in0=v, scalar=SLOPE, in1=v, op0=ALU.mult, op1=ALU.max)
+
+        def leaky_plain(u):
+            new_f(u, "2")
+            v = y[u, "2"][:]
+            nc.vector.scalar_tensor_tensor(out=f[u, "2"][:], in0=v, scalar=SLOPE, in1=v, op0=ALU.mult, op1=ALU.max)
 
         def flip(u):
-            f = fs[u, 2]
-            s4 = sgnb[:, u, :].unsqueeze(1).to_broadcast([P, 512, 4])
-            nc.vector.tensor_tensor(out=f[:], in0=f[:], in1=s4, op=ALU.mult)
+            s4 = sgnb[:, u, :].unsqueeze(1).to_broadcast([P, N, T])
+            nc.vector.tensor_tensor(out=f[u, "2"][:], in0=f[u, "2"][:], in1=s4, op=ALU.mult)
 
-        def quant_f(u, k):
-            c = keep.tile([P, 512], U32, name="fc%d_%d" % (u, k), align_bytes=256)
-            s = keep.tile([P, 512], U8, name="fs%d_%d" % (u, k), align_bytes=256)
-            nc.vector.quantize_mx(
-                out=c[:].bitcast(FP8X4), scales=s[:], in_=fs[u, k][:].rearrange("p c t -> p (c t)")
-            )
-            fq[u, k] = (c, s)
+        def signed(u):
+            return u >= 2
+
+        def z2(u):
+            for q in range(4):
+                (z2_signed if signed(u) else z2_plain)(u, q)
 
         def gram(b, i):
-            g = ps_z.tile([P, C2], F32, name="z") if b == 1 else ps_g.tile([P, C2], F32, name="g")
+            g = ps_z.tile([P, N], F32, name="z") if b == 1 else ps_g.tile([P, N], F32, name="g")
             for n in range(2):
                 u = 2 * b + n
-                mm(g[:], fq[u, i // 4], (i % 4) * P, fq[u, 2][0][:].bitcast(FP8X4), fq[u, 2][1][:], n == 0, n == 1)
-            e = ep.tile([P, C2], F32, name="e")
-            es[b, i] = e
-            nc.vector.scalar_tensor_tensor(
-                out=e[:], in0=g[:], scalar=1.0 / 32.0, in1=a_sb[b][:, i, :], op0=ALU.mult, op1=ALU.subtract
-            )
+                mx(g[:], fq[u, i // 4], (i % 4) * P, fq[u, "2"][0][:].bitcast(FP8X4), fq[u, "2"][1][:], n == 0, n == 1)
+            e[b, i] = ep.tile([P, N], F32, name="e")
+            ev, gv, av = e[b, i][:], g[:], a_sb[b][:, i // 4, i % 4, :]
+            if signed(2 * b):
+                ev = ev.rearrange("p (c i) -> p c i", i=4)
+                gv = gv.rearrange("p (i c) -> p c i", i=4)
+                av = av.rearrange("p (c i) -> p c i", i=4)
+            w = ev.shape[1] // parts(b, i)
+            for c in range(0, ev.shape[1], w):
+                nc.vector.scalar_tensor_tensor(
+                    out=ev[:, c : c + w], in0=gv[:, c : c + w], scalar=1.0 / 32.0, in1=av[:, c : c + w],
+                    op0=ALU.mult, op1=ALU.subtract
+                )
 
         def finish(b, i):
-            e = es[b, i]
-            nc.scalar.activation(out=e[:], in_=e[:], func=ACT.Tanh)
-            nc.sync.dma_start(out=out[b, P * i : P * i + P, :], in_=e[:])
+            rows = out[b].rearrange("(h p i) n -> p h i n", p=P, i=4)[:, i // 4, i % 4, :]
+            w = N // parts(b, i)
+            for c in range(0, N, w):
+                nc.scalar.activation(out=e[b, i][:, c : c + w], in_=e[b, i][:, c : c + w], func=ACT.Tanh)
+                nc.sync.dma_start(out=rows[:, c : c + w], in_=e[b, i][:, c : c + w])
 
+        def parts(b, i):
+            return 2 if (b, i) == (B - 1, 7) else 1
+
+        keep_warm(3)
+        spread_scales()
+        keep_warm(3)
         widen(0)
-        turn_x2(0)
-        quant_x2(0)
-        nc.vector.tensor_scalar(out=sgn[:], in0=m_sb[:], scalar1=0.0, scalar2=2.0, op0=ALU.is_ge, op1=ALU.mult)
-        nc.vector.tensor_scalar(out=sgn[:], in0=sgn[:], scalar1=-1.0, scalar2=None, op0=ALU.add)
-        nc.vector.tensor_tensor(out=mag[:], in0=m_sb[:], in1=sgn[:], op=ALU.mult)
-        nc.vector.tensor_copy(out=sgnb[:], in_=sgn[:])
-        nc.vector.tensor_scalar(out=mag5[:], in0=mag[:], scalar1=SLOPE, scalar2=None, op0=ALU.mult)
-        turn_x1(0)
-        quant_x1(0)
+        turn_x2(0, 0)
+        turn_x2(0, 1)
+        keep_warm(2)
+        turn_x2(0, 2)
+        turn_x2(0, 3)
+        quantize_x2(0, 0)
+        quantize_x2(0, 1)
+        split_m()
+        keep_warm(1)
+        turn_x1(0, 0)
+        turn_x1(0, 1)
+        quantize_x1(0)
         widen(1)
         z2(0)
 
-        todo = []
+        waiting, open_tiles = [], []
 
-        def next_gram():
-            if todo:
-                gram(*todo[0])
+        def gram_next(k):
+            for i in range(k):
+                gram(*waiting[0])
+                open_tiles.append(waiting.pop(0))
 
-        def next_finish():
-            if todo:
-                finish(*todo[0])
-                todo.remove(todo[0])
+        def finish_next():
+            if open_tiles:
+                finish(*open_tiles.pop(0))
 
         for u in range(UNITS):
-            more = u + 1 < UNITS
-            z1(u, 0)
-            leaky(u, 2)
-            next_gram()
-            if more:
-                turn_x2(u + 1)
-            next_finish()
+            nxt = u + 1 if u + 1 < UNITS else None
+            share = EPILOGUE.get(u, (0, 0, 0, 0, 0))
+            gram_next(share[0])
+            for t in range(T):
+                z1(u, 0, t)
+                if t == 1 and nxt:
+                    turn_x2(nxt, 0)
+            if signed(u):
+                leaky(u, "2")
+            else:
+                leaky_plain(u)
+            gram_next(share[1])
+            if nxt:
+                for t in range(1, T):
+                    turn_x2(nxt, t)
+            if not signed(u):
+                flip(u)
+            gram_next(share[2])
             leaky(u, 0)
-            if more:
-                quant_x2(u + 1)
-            z1(u, 1)
-            flip(u)
-            next_gram()
+            if nxt:
+                quantize_x2(nxt, 0)
+                quantize_x2(nxt, 1)
+            for t in range(T):
+                z1(u, 1, t)
+            gram_next(share[3])
+            finish_next()
+            quantize_f(u, "2")
+            quantize_f(u, 0)
             leaky(u, 1)
-            quant_f(u, 2)
-            next_finish()
-            if more:
-                turn_x1(u + 1)
-                quant_x1(u + 1)
-            quant_f(u, 0)
-            next_gram()
-            if more:
-                z2(u + 1)
-            next_finish()
+            if nxt:
+                turn_x1(nxt, 0)
+                turn_x1(nxt, 1)
+                quantize_x1(nxt)
+            gram_next(share[4])
+            if nxt:
+                z2(nxt)
+            finish_next()
             if u + 2 < UNITS:
                 widen(u + 2)
-            next_gram()
-            quant_f(u, 1)
-            next_finish()
             if u % 2 == 1:
-                todo.extend([(u // 2, i) for i in range(8)])
-        for i in range(4):
-            gram(1, i)
-            if i > 0:
-                finish(1, i - 1)
-        for i in range(4, 8):
-            gram(1, i)
-            finish(1, i - 1)
-        finish(1, 7)
+                waiting += [(u // 2, i) for i in range(8)]
+            if u == UNITS - 1:
+                gram_next(2)
+            quantize_f(u, 1)
+            finish_next()
+        for i in range(6):
+            finish_next()
+            gram_next(1)
+        for i in range(len(open_tiles)):
+            finish_next()

@@ -22,6 +22,7 @@ K_PASS = P * T
 N = 512
 UNITS = B * S // K_PASS
 SLOPE = 0.2
+TWICE = (1, 2, 3)
 EPILOGUE = {2: (0, 1, 0, 1, 0), 3: (2, 0, 2, 1, 1)}
 
 
@@ -34,7 +35,7 @@ def tile_crosslayerguidedstylegramlogcoshgrad_w4_kernel(
         xp = ctx.enter_context(tc.tile_pool(name="xp", bufs=UNITS))
         wp = ctx.enter_context(tc.tile_pool(name="wp", bufs=2))
         yp = ctx.enter_context(tc.tile_pool(name="yp", bufs=3))
-        up = ctx.enter_context(tc.tile_pool(name="up", bufs=2))
+        pp = ctx.enter_context(tc.tile_pool(name="pp", bufs=2))
         fp = ctx.enter_context(tc.tile_pool(name="fp", bufs=3))
         ep = ctx.enter_context(tc.tile_pool(name="ep", bufs=8))
         ps_t = ctx.enter_context(tc.psum_pool(name="ps_t", bufs=2))
@@ -97,7 +98,7 @@ def tile_crosslayerguidedstylegramlogcoshgrad_w4_kernel(
         sgn = keep.tile([P, UNITS, T], F32, name="sgn")
         mag = keep.tile([P, UNITS, T], F32, name="mag")
         sgnb = keep.tile([P, UNITS, T], BF16, name="sgnb")
-        x1w, x1g, x2g, x1q, x2q, y, uu, f, fq, e = {}, {}, {}, {}, {}, {}, {}, {}, {}, {}
+        x1w, x1g, x2g, x1q, x2q, y, low, f, fq, e = {}, {}, {}, {}, {}, {}, {}, {}, {}, {}
 
         def keep_warm(n):
             for i in range(n):
@@ -168,28 +169,23 @@ def tile_crosslayerguidedstylegramlogcoshgrad_w4_kernel(
                 rhs=words, rhs_scale=scales, start=start, stop=stop,
             )
 
-        def z2_plain(u, q):
+        def z2(u, q):
+            twice = u in TWICE
             if q == 0:
-                y[u, "2"] = yp.tile([P, N, T], F32, name="y")
+                y[u, "2"] = pp.tile([P, N, T], BF16, name="yb") if twice else yp.tile([P, N, T], F32, name="y")
+                if twice:
+                    low[u] = pp.tile([P, N, T], BF16, name="low")
             z = ps_z.tile([P, T, P], F32, name="z")
             for t in range(T):
                 for g in range(2):
                     mx(z[:, t, :], x2q[u, t // 2], (2 * (t % 2) + g) * P,
                        w2c[:, g, 2 * P * q : 2 * P * q + 2 * P].bitcast(FP4X4),
                        ws[:, C1 + C2 * g + P * q : C1 + C2 * g + P * q + P], g == 0, g == 1)
-            nc.scalar.copy(out=y[u, "2"][:, P * q : P * q + P, :], in_=z[:].rearrange("p t c -> p c t"))
-
-        def z2_signed(u, t):
-            if t == 0:
-                y[u, "2"] = yp.tile([P, P, T, 4], F32, name="y")
-                uu[u] = up.tile([P, P, T, 4], F32, name="v")
-            z = ps_z.tile([P, N], F32, name="z")
-            for g in range(2):
-                mx(z[:], x2q[u, t // 2], (2 * (t % 2) + g) * P, w2c[:, g, :].bitcast(FP4X4),
-                   ws[:, C1 + C2 * g : C1 + C2 * g + C2], g == 0, g == 1)
-            zv = z[:].rearrange("p (c i) -> p c i", i=4)
-            nc.scalar.activation(out=uu[u][:, :, t, :], in_=zv, func=ACT.Sign)
-            nc.scalar.activation(out=y[u, "2"][:, :, t, :], in_=zv, func=ACT.Copy, scale=sgn[:, u, t : t + 1])
+            zv = z[:].rearrange("p t c -> p c t")
+            cols = slice(P * q, P * q + P)
+            nc.scalar.copy(out=y[u, "2"][:, cols, :], in_=zv)
+            if twice:
+                nc.scalar.activation(out=low[u][:, cols, :], in_=zv, func=ACT.Copy, scale=SLOPE)
 
         def z1(u, h, t):
             if t == 0:
@@ -202,34 +198,23 @@ def tile_crosslayerguidedstylegramlogcoshgrad_w4_kernel(
                 scale=mag[:, u, t : t + 1],
             )
 
-        def new_f(u, k):
-            f[u, k] = fp.tile([P, N, T], BF16, name="f", align_bytes=64)
-            return f[u, k][:].rearrange("p c t -> p (c t)").rearrange("p (i n) -> p n i", i=4)
+        def leaky(u, h):
+            f[u, h] = fp.tile([P, N, T], BF16, name="f", align_bytes=64)
+            o = f[u, h][:].rearrange("p c t -> p (c t)").rearrange("p (i n) -> p n i", i=4)
+            v = y[u, h][:].rearrange("p c t i -> p (c t) i")
+            nc.vector.scalar_tensor_tensor(out=o, in0=v, scalar=SLOPE, in1=v, op0=ALU.mult, op1=ALU.max)
 
-        def leaky(u, k):
-            o = new_f(u, k)
-            v = y[u, k][:].rearrange("p c t i -> p (c t) i")
-            if k == "2":
-                s = uu[u][:].rearrange("p c t i -> p (c t) i")
-                nc.vector.scalar_tensor_tensor(out=o, in0=s, scalar=SLOPE, in1=v, op0=ALU.max, op1=ALU.mult)
-            else:
-                nc.vector.scalar_tensor_tensor(out=o, in0=v, scalar=SLOPE, in1=v, op0=ALU.mult, op1=ALU.max)
-
-        def leaky_plain(u):
-            new_f(u, "2")
+        def leaky_2(u):
+            f[u, "2"] = fp.tile([P, N, T], BF16, name="f", align_bytes=64)
             v = y[u, "2"][:]
-            nc.vector.scalar_tensor_tensor(out=f[u, "2"][:], in0=v, scalar=SLOPE, in1=v, op0=ALU.mult, op1=ALU.max)
+            if u in TWICE:
+                nc.vector.tensor_tensor(out=f[u, "2"][:], in0=v, in1=low[u][:], op=ALU.max)
+            else:
+                nc.vector.scalar_tensor_tensor(out=f[u, "2"][:], in0=v, scalar=SLOPE, in1=v, op0=ALU.mult, op1=ALU.max)
 
         def flip(u):
             s4 = sgnb[:, u, :].unsqueeze(1).to_broadcast([P, N, T])
             nc.vector.tensor_tensor(out=f[u, "2"][:], in0=f[u, "2"][:], in1=s4, op=ALU.mult)
-
-        def signed(u):
-            return u >= 2
-
-        def z2(u):
-            for q in range(4):
-                (z2_signed if signed(u) else z2_plain)(u, q)
 
         def gram(b, i):
             g = ps_z.tile([P, N], F32, name="z") if b == 1 else ps_g.tile([P, N], F32, name="g")
@@ -238,10 +223,6 @@ def tile_crosslayerguidedstylegramlogcoshgrad_w4_kernel(
                 mx(g[:], fq[u, i // 4], (i % 4) * P, fq[u, "2"][0][:].bitcast(FP8X4), fq[u, "2"][1][:], n == 0, n == 1)
             e[b, i] = ep.tile([P, N], F32, name="e")
             ev, gv, av = e[b, i][:], g[:], a_sb[b][:, i // 4, i % 4, :]
-            if signed(2 * b):
-                ev = ev.rearrange("p (c i) -> p c i", i=4)
-                gv = gv.rearrange("p (i c) -> p c i", i=4)
-                av = av.rearrange("p (c i) -> p c i", i=4)
             w = ev.shape[1] // parts(b, i)
             for c in range(0, ev.shape[1], w):
                 nc.vector.scalar_tensor_tensor(
@@ -276,7 +257,8 @@ def tile_crosslayerguidedstylegramlogcoshgrad_w4_kernel(
         turn_x1(0, 1)
         quantize_x1(0)
         widen(1)
-        z2(0)
+        for q in range(4):
+            z2(0, q)
 
         waiting, open_tiles = [], []
 
@@ -297,18 +279,17 @@ def tile_crosslayerguidedstylegramlogcoshgrad_w4_kernel(
                 z1(u, 0, t)
                 if t == 1 and nxt:
                     turn_x2(nxt, 0)
-            if signed(u):
-                leaky(u, "2")
-            else:
-                leaky_plain(u)
+            leaky_2(u)
             gram_next(share[1])
             if nxt:
                 for t in range(1, T):
                     turn_x2(nxt, t)
-            if not signed(u):
-                flip(u)
             gram_next(share[2])
+            if u == 0:
+                flip(u)
             leaky(u, 0)
+            if u > 0:
+                flip(u)
             if nxt:
                 quantize_x2(nxt, 0)
                 quantize_x2(nxt, 1)
@@ -316,8 +297,8 @@ def tile_crosslayerguidedstylegramlogcoshgrad_w4_kernel(
                 z1(u, 1, t)
             gram_next(share[3])
             finish_next()
-            quantize_f(u, "2")
             quantize_f(u, 0)
+            quantize_f(u, "2")
             leaky(u, 1)
             if nxt:
                 turn_x1(nxt, 0)
@@ -325,7 +306,8 @@ def tile_crosslayerguidedstylegramlogcoshgrad_w4_kernel(
                 quantize_x1(nxt)
             gram_next(share[4])
             if nxt:
-                z2(nxt)
+                for q in range(4):
+                    z2(nxt, q)
             finish_next()
             if u + 2 < UNITS:
                 widen(u + 2)

from contextlib import ExitStack

import concourse.mybir as mybir
from concourse.masks import make_identity

F32 = mybir.dt.float32
BF16 = mybir.dt.bfloat16
U32 = mybir.dt.uint32
I32 = mybir.dt.int32
U8 = mybir.dt.uint8
FP8 = mybir.dt.float8_e4m3fn
FP8X4 = mybir.dt.float8_e4m3fn_x4
FP4X4 = mybir.dt.float4_e2m1fn_x4
ALU = mybir.AluOpType
ACT = mybir.ActivationFunctionType

B, S, D1, D2, C1, C2 = 2, 1024, 512, 1024, 1024, 512
FLOPS = 2 * B * S * (D1 * C1 + D2 * C2 + C1 * C2)
P = 128
T = 4
K_PASS = P * T
N = 512
UNITS = B * S // K_PASS
SLOPE = 0.2
TWICE = (1, 2, 3)
EPILOGUE = {2: (0, 1, 0, 1, 0), 3: (2, 0, 2, 1, 1)}


def tile_crosslayerguidedstylegramlogcoshgrad_w4_kernel(
    tc, x1_bytes, x1_scale, x2, w1_words, w1_scales, w2_words, w2_scales, m, a, out
):
    nc = tc.nc
    with ExitStack() as ctx:
        keep = ctx.enter_context(tc.tile_pool(name="keep", bufs=1))
        xp = ctx.enter_context(tc.tile_pool(name="xp", bufs=UNITS))
        wp = ctx.enter_context(tc.tile_pool(name="wp", bufs=2))
        yp = ctx.enter_context(tc.tile_pool(name="yp", bufs=3))
        pp = ctx.enter_context(tc.tile_pool(name="pp", bufs=2))
        fp = ctx.enter_context(tc.tile_pool(name="fp", bufs=3))
        ep = ctx.enter_context(tc.tile_pool(name="ep", bufs=8))
        ps_t = ctx.enter_context(tc.psum_pool(name="ps_t", bufs=2))
        ps_z = ctx.enter_context(tc.psum_pool(name="ps_z", bufs=4))
        ps_g = ctx.enter_context(tc.psum_pool(name="ps_g", bufs=2))

        zb = keep.tile([P, N], BF16, name="zb")
        nc.gpsimd.memset(zb[:], 0.0)
        ident = keep.tile([P, P], F32, name="ident")
        make_identity(nc, ident[:])

        ctx.enter_context(tc.manual_schedule())

        sct = keep.tile([P, T], F32, name="sct")
        nc.scalar.dma_start(out=sct[:], in_=x1_scale.rearrange("o q (p j) -> p (o q j)", j=T))
        warm = keep.tile([P, 1], F32, name="warm")
        nc.vector.memset(warm[:], 0.0)
        nc.scalar.activation(out=warm[:], in_=warm[:], func=ACT.Tanh)

        w1c = keep.tile([P, 2 * C1], U8, name="w1c", align_bytes=256)
        w2c = keep.tile([P, 2, 2 * C2], U8, name="w2c", align_bytes=256)
        ws = keep.tile([P, C1 + 2 * C2], U8, name="ws", align_bytes=256)
        nc.vector.memset(ws[:].bitcast(I32), 0)
        m_sb = keep.tile([P, UNITS, T], BF16, name="m_sb")
        a_sb = [keep.tile([P, 2, T, C2], BF16, name="a_sb%d" % b) for b in range(B)]
        x1b = [xp.tile([P, T, D1], U8, name="x1b") for u in range(UNITS)]
        x2b = [xp.tile([P, T, D2], BF16, name="x2b") for u in range(UNITS)]

        def unit_rows(x, u):
            return x[u // 2, K_PASS * (u % 2) : K_PASS * (u % 2) + K_PASS, :].rearrange("(p t) k -> p t k", t=T)

        def load_x1(u):
            nc.sync.dma_start(out=x1b[u][:], in_=unit_rows(x1_bytes, u))

        def load_x2(u, t0, t1):
            nc.sync.dma_start(out=x2b[u][:, t0:t1, :], in_=unit_rows(x2, u)[:, t0:t1, :])

        load_x1(0)
        load_x2(0, 0, 2)
        load_x2(0, 2, 4)
        nc.sync.dma_start(out=m_sb[:], in_=m.rearrange("b (g p t) -> p (b g) t", p=P, t=T))
        nc.sync.dma_start(out=w2c[:].bitcast(I32), in_=w2_words.rearrange("g p n -> p g n").bitcast(I32))
        for q in range(4):
            nc.sync.dma_start(
                out=ws[32 * q : 32 * q + 4, C1:].rearrange("p (g n) -> p g n", g=2).bitcast(I32),
                in_=w2_scales[:, 4 * q : 4 * q + 4, :].rearrange("g q n -> q g n").bitcast(I32),
            )
        for q in range(4):
            nc.sync.dma_start(
                out=ws[32 * q : 32 * q + 4, 0:C1].bitcast(I32), in_=w1_scales[0, 4 * q : 4 * q + 4, :].bitcast(I32)
            )
        nc.sync.dma_start(out=w1c[:].bitcast(I32), in_=w1_words[0].bitcast(I32))
        for u in range(1, UNITS):
            load_x1(u)
            load_x2(u, 0, 4)
            if u >= 2:
                nc.sync.dma_start(out=a_sb[u - 2][:], in_=a[u - 2].rearrange("(h p i) n -> p h i n", p=P, i=T))

        sc = keep.tile([P, P, T], F32, name="sc")
        sgn = keep.tile([P, UNITS, T], F32, name="sgn")
        mag = keep.tile([P, UNITS, T], F32, name="mag")
        sgnb = keep.tile([P, UNITS, T], BF16, name="sgnb")
        x1w, x1g, x2g, x1q, x2q, y, low, f, fq, e = {}, {}, {}, {}, {}, {}, {}, {}, {}, {}

        def keep_warm(n):
            for i in range(n):
                g = ps_g.tile([P, N], F32, name="g")
                nc.tensor.matmul(g[:], lhsT=zb[:, 0:P], rhs=zb[:], start=True, stop=True)

        def spread_scales():
            tr = ps_t.tile([P, T, P], F32, name="tr")
            for j in range(T):
                nc.tensor.transpose(tr[:, j, :], sct[:, j : j + 1].to_broadcast([P, P]), ident[:])
            nc.vector.tensor_copy(out=sc[:], in_=tr[:].rearrange("p j n -> p n j"))

        def split_m():
            nc.vector.tensor_scalar(out=sgn[:], in0=m_sb[:], scalar1=0.0, scalar2=2.0, op0=ALU.is_ge, op1=ALU.mult)
            nc.vector.tensor_scalar(out=sgn[:], in0=sgn[:], scalar1=-1.0, scalar2=None, op0=ALU.add)
            nc.vector.tensor_tensor(out=mag[:], in0=m_sb[:], in1=sgn[:], op=ALU.mult)
            nc.vector.tensor_copy(out=sgnb[:], in_=sgn[:])

        def widen(u):
            w = wp.tile([P, T, D1], BF16, name="x1w", align_bytes=64)
            x1w[u] = w
            for t in range(T):
                nc.vector.tensor_tensor(
                    out=w[:, t, :], in0=x1b[u][:, t, :].bitcast(FP8), in1=sc[:].rearrange("p n j -> p (n j)"), op=ALU.mult
                )

        def turn_x2(u, t):
            if t == 0:
                x2g[u] = wp.tile([P, T, 2, P, T], BF16, name="x2g", align_bytes=64)
            words = x2b[u][:, t, :].bitcast(F32)
            tr = ps_t.tile([P, T, P], F32, name="tr")
            for j in range(4):
                k0 = 256 * (j // 2)
                nc.tensor.transpose(tr[:, j, :], words[:, k0 + j % 2 : k0 + 256 : 2], ident[:])
            nc.scalar.copy(out=x2g[u][:, t].bitcast(F32), in_=tr[:].rearrange("p (g e) r -> p g r e", e=2))

        def turn_x1(u, h):
            if h == 0:
                x1g[u] = wp.tile([P, T, P, T], BF16, name="x1g", align_bytes=64)
            tr = ps_t.tile([P, T, P], F32, name="tr")
            for j in range(4):
                words = x1w[u][:, 2 * h + j // 2, :].bitcast(F32)
                nc.tensor.transpose(tr[:, j, :], words[:, j % 2 : 256 : 2], ident[:])
            nc.scalar.copy(
                out=x1g[u][:, 2 * h : 2 * h + 2].bitcast(F32), in_=tr[:].rearrange("p (t e) r -> p t r e", e=2)
            )

        def quantize(pool, src, names):
            c = pool.tile([P, N], U32, name=names[0], align_bytes=256)
            s = pool.tile([P, N], U8, name=names[1], align_bytes=256)
            nc.vector.quantize_mx(out=c[:].bitcast(FP8X4), scales=s[:], in_=src)
            return c, s

        def quantize_x2(u, h):
            x2q[u, h] = quantize(
                fp, x2g[u][:, 2 * h : 2 * h + 2].rearrange("p t g r k -> p (t g r k)"), ("x2c%d" % h, "x2s%d" % h)
            )

        def quantize_x1(u):
            x1q[u] = quantize(fp, x1g[u][:].rearrange("p t r k -> p (t r k)"), ("x1c", "x1s"))

        def quantize_f(u, k):
            fq[u, k] = quantize(keep, f[u, k][:].rearrange("p c t -> p (c t)"), ("fc%d%s" % (u, k), "fs%d%s" % (u, k)))

        def mx(o, left, col, words, scales, start, stop):
            nc.tensor.matmul_mx(
                out=o, lhsT=left[0][:, col : col + P].bitcast(FP8X4), lhsT_scale=left[1][:, col : col + P],
                rhs=words, rhs_scale=scales, start=start, stop=stop,
            )

        def z2(u, q):
            twice = u in TWICE
            if q == 0:
                y[u, "2"] = pp.tile([P, N, T], BF16, name="yb") if twice else yp.tile([P, N, T], F32, name="y")
                if twice:
                    low[u] = pp.tile([P, N, T], BF16, name="low")
            z = ps_z.tile([P, T, P], F32, name="z")
            for t in range(T):
                for g in range(2):
                    mx(z[:, t, :], x2q[u, t // 2], (2 * (t % 2) + g) * P,
                       w2c[:, g, 2 * P * q : 2 * P * q + 2 * P].bitcast(FP4X4),
                       ws[:, C1 + C2 * g + P * q : C1 + C2 * g + P * q + P], g == 0, g == 1)
            zv = z[:].rearrange("p t c -> p c t")
            cols = slice(P * q, P * q + P)
            nc.scalar.copy(out=y[u, "2"][:, cols, :], in_=zv)
            if twice:
                nc.scalar.activation(out=low[u][:, cols, :], in_=zv, func=ACT.Copy, scale=SLOPE)

        def z1(u, h, t):
            if t == 0:
                y[u, h] = yp.tile([P, P, T, 4], F32, name="y")
            z = ps_z.tile([P, N], F32, name="z")
            mx(z[:], x1q[u], t * P, w1c[:, 2 * N * h : 2 * N * h + 2 * N].bitcast(FP4X4), ws[:, N * h : N * h + N],
               True, True)
            nc.scalar.activation(
                out=y[u, h][:, :, t, :], in_=z[:].rearrange("p (c i) -> p c i", i=4), func=ACT.Copy,
                scale=mag[:, u, t : t + 1],
            )

        def leaky(u, h):
            f[u, h] = fp.tile([P, N, T], BF16, name="f", align_bytes=64)
            o = f[u, h][:].rearrange("p c t -> p (c t)").rearrange("p (i n) -> p n i", i=4)
            v = y[u, h][:].rearrange("p c t i -> p (c t) i")
            nc.vector.scalar_tensor_tensor(out=o, in0=v, scalar=SLOPE, in1=v, op0=ALU.mult, op1=ALU.max)

        def leaky_2(u):
            f[u, "2"] = fp.tile([P, N, T], BF16, name="f", align_bytes=64)
            v = y[u, "2"][:]
            if u in TWICE:
                nc.vector.tensor_tensor(out=f[u, "2"][:], in0=v, in1=low[u][:], op=ALU.max)
            else:
                nc.vector.scalar_tensor_tensor(out=f[u, "2"][:], in0=v, scalar=SLOPE, in1=v, op0=ALU.mult, op1=ALU.max)

        def flip(u):
            s4 = sgnb[:, u, :].unsqueeze(1).to_broadcast([P, N, T])
            nc.vector.tensor_tensor(out=f[u, "2"][:], in0=f[u, "2"][:], in1=s4, op=ALU.mult)

        def gram(b, i):
            g = ps_z.tile([P, N], F32, name="z") if b == 1 else ps_g.tile([P, N], F32, name="g")
            for n in range(2):
                u = 2 * b + n
                mx(g[:], fq[u, i // 4], (i % 4) * P, fq[u, "2"][0][:].bitcast(FP8X4), fq[u, "2"][1][:], n == 0, n == 1)
            e[b, i] = ep.tile([P, N], F32, name="e")
            ev, gv, av = e[b, i][:], g[:], a_sb[b][:, i // 4, i % 4, :]
            w = ev.shape[1] // parts(b, i)
            for c in range(0, ev.shape[1], w):
                nc.vector.scalar_tensor_tensor(
                    out=ev[:, c : c + w], in0=gv[:, c : c + w], scalar=1.0 / 32.0, in1=av[:, c : c + w],
                    op0=ALU.mult, op1=ALU.subtract
                )

        def finish(b, i):
            rows = out[b].rearrange("(h p i) n -> p h i n", p=P, i=4)[:, i // 4, i % 4, :]
            w = N // parts(b, i)
            for c in range(0, N, w):
                nc.scalar.activation(out=e[b, i][:, c : c + w], in_=e[b, i][:, c : c + w], func=ACT.Tanh)
                nc.sync.dma_start(out=rows[:, c : c + w], in_=e[b, i][:, c : c + w])

        def parts(b, i):
            return 2 if (b, i) == (B - 1, 7) else 1

        keep_warm(3)
        spread_scales()
        keep_warm(3)
        widen(0)
        turn_x2(0, 0)
        turn_x2(0, 1)
        keep_warm(2)
        turn_x2(0, 2)
        turn_x2(0, 3)
        quantize_x2(0, 0)
        quantize_x2(0, 1)
        split_m()
        keep_warm(1)
        turn_x1(0, 0)
        turn_x1(0, 1)
        quantize_x1(0)
        widen(1)
        for q in range(4):
            z2(0, q)

        waiting, open_tiles = [], []

        def gram_next(k):
            for i in range(k):
                gram(*waiting[0])
                open_tiles.append(waiting.pop(0))

        def finish_next():
            if open_tiles:
                finish(*open_tiles.pop(0))

        for u in range(UNITS):
            nxt = u + 1 if u + 1 < UNITS else None
            share = EPILOGUE.get(u, (0, 0, 0, 0, 0))
            gram_next(share[0])
            for t in range(T):
                z1(u, 0, t)
                if t == 1 and nxt:
                    turn_x2(nxt, 0)
            leaky_2(u)
            gram_next(share[1])
            if nxt:
                for t in range(1, T):
                    turn_x2(nxt, t)
            gram_next(share[2])
            if u == 0:
                flip(u)
            leaky(u, 0)
            if u > 0:
                flip(u)
            if nxt:
                quantize_x2(nxt, 0)
                quantize_x2(nxt, 1)
            for t in range(T):
                z1(u, 1, t)
            gram_next(share[3])
            finish_next()
            quantize_f(u, 0)
            quantize_f(u, "2")
            leaky(u, 1)
            if nxt:
                turn_x1(nxt, 0)
                turn_x1(nxt, 1)
                quantize_x1(nxt)
            gram_next(share[4])
            if nxt:
                for q in range(4):
                    z2(nxt, q)
            finish_next()
            if u + 2 < UNITS:
                widen(u + 2)
            if u % 2 == 1:
                waiting += [(u // 2, i) for i in range(8)]
            if u == UNITS - 1:
                gram_next(2)
            quantize_f(u, 1)
            finish_next()
        for i in range(6):
            finish_next()
            gram_next(1)
        for i in range(len(open_tiles)):
            finish_next()
